import numpy as np
import ml_dtypes


def mxq(x, axis, fmt="e4m3"):
    dtype, down = {"e4m3": (ml_dtypes.float8_e4m3fn, 7), "e5m2": (ml_dtypes.float8_e5m2, 14)}[fmt]
    v = np.moveaxis(np.asarray(x, np.float32).astype(ml_dtypes.bfloat16).astype(np.float64), axis, -1)
    blocks = v.reshape(v.shape[:-1] + (-1, 32))
    amax = np.abs(blocks).max(-1, keepdims=True)
    byte = np.maximum(np.where(amax > 0, np.frexp(amax)[1] - 1 + 127, 0) - down, 1)
    scale = np.exp2(byte - 127.0)
    codes = (blocks / scale).astype(np.float32).astype(dtype).astype(np.float64)
    return np.moveaxis((codes * scale).reshape(v.shape), -1, axis)


WIDE = False


def mx_kscale(k):
    if not WIDE:
        return np.ones(k)
    levels = np.array([10, -10, 5, -5, 0])
    if k % 512:
        return np.exp2(np.random.permutation(np.resize(levels, k // 32))).repeat(32)
    a = np.empty((k // 512, 16))
    for p in range(k // 512):
        a[p, :8] = np.random.permutation(np.resize(levels, 8))
        for g in range(8):
            far = levels[np.abs(levels - a[p, g]) >= 10]
            a[p, g + 8] = far[np.random.randint(len(far))]
    return np.exp2(a.ravel()).repeat(32)


def f64(x):
    return np.asarray(x).astype(np.float64)


def striped(idx):
    return np.tile(idx.reshape(-1, 16).T, (8, 1)).astype(np.uint16)


def unstriped(offs):
    return offs[:16].T.reshape(-1).astype(np.int64)


def striped8(idx):
    return np.concatenate([x.reshape(-1, 16).T for x in idx]).astype(np.uint16)


def runs(offs, k):
    lists = np.stack([offs[16 * r : 16 * r + 16].T.reshape(-1) for r in range(8)]).astype(np.int64)
    return lists[np.arange(k) % 512 // 64]


def pack_weight(w):
    k, n = w.shape
    w = f64(np.asarray(w, np.float32).astype(ml_dtypes.bfloat16)).reshape(k // 32, 32, n)
    amax = np.abs(w).max(1)
    byte = np.clip(np.where(amax > 0, np.frexp(amax)[1] - 1 + 127 - 7, 1), 1, 254)
    scaled = (w * np.exp2(127.0 - byte)[:, None, :]).reshape(k, n).astype(np.float32)
    words = np.ascontiguousarray(scaled.reshape(k // 512, 128, 4, n).transpose(0, 1, 3, 2)).astype(ml_dtypes.float8_e4m3fn).view(np.uint8)
    return words, np.ascontiguousarray(byte.astype(np.uint8).reshape(k // 512, 16, n))


def unpack_weight(words, scales):
    g, p, n, _ = words.shape
    vals = np.ascontiguousarray(words).view(ml_dtypes.float8_e4m3fn).astype(np.float64) * np.repeat(np.exp2(scales.astype(np.float64) - 127.0), 8, axis=1)[..., None]
    return vals.transpose(0, 1, 3, 2).reshape(g * 512, n)

def planes(y):
    n, m = y.shape
    v = y.astype(np.float32).astype(ml_dtypes.bfloat16).astype(np.float64).reshape(n // 32, 32, m)
    top = np.abs(v).max(1)
    byte = np.clip(np.where(top > 0, np.frexp(top)[1] - 1 + 127 - 7, 1), 1, 254)
    codes = (v * np.exp2(127.0 - byte)[:, None, :]).reshape(n, m).astype(np.float32).astype(ml_dtypes.float8_e4m3fn).view(np.uint8)
    words = codes.reshape(n // 512, 128, 4, m).transpose(0, 1, 3, 2)
    return np.ascontiguousarray(words), np.ascontiguousarray(byte.astype(np.uint8).reshape(n // 512, 16, m))


K, T, S, N, H = 512, 2048, 512, 512, 512


def setup_inputs():
    n = np.random.standard_normal
    s = mx_kscale(K)[:, None]
    u = mx_kscale(S)
    packed_xT = pack_weight(n((K, T)) * s)
    return {
        "x_words": packed_xT[0],
        "x_scales": packed_xT[1],
        "wa": (n((K, H)) / np.sqrt(K) / s).astype(np.float32),
        "wb": (n((K, N)) / np.sqrt(K) / s).astype(np.float32),
        "gt": (np.random.uniform(0.5, 1.5, (S, 1)) * u[:, None]).astype(np.float32),
        "gi": (np.random.uniform(0.5, 1.5, (S, 1)) / u[:, None]).astype(np.float32),
        "offs": striped(np.random.permutation(T)[:S]),
        "two": striped(np.random.permutation(T)[:S]),
        "fa": striped8(np.stack([np.random.permutation(H) for _ in range(8)])),
        "nb": striped8(np.stack([np.random.permutation(N) for _ in range(8)])),
    }


def reference(x_words, x_scales, wa, wb, gt, gi, offs, two, fa, nb):
    xq = unpack_weight(x_words, x_scales)[:, unstriped(offs)]
    a = xq.T @ mxq(f64(wa), 0, "e4m3")
    z = f64(gt) * (np.maximum(a, a[np.arange(S)[:, None], runs(fa, S)]))
    x_two = unpack_weight(x_words, x_scales)[:, unstriped(two)]
    b = x_two.T @ mxq(f64(wb), 0, "e4m3")
    z2 = f64(gi) * b
    cv = 0.0625 * ((mxq(z, 0, "e4m3").T @ mxq(z2, 0, "e4m3")))
    out_0 = np.maximum(cv, cv[np.arange(H)[:, None], runs(nb, H)])
    return (out_0,) + planes(out_0)

@@ -1,0 +1,222 @@
+from contextlib import ExitStack
+
+import concourse.mybir as mybir
+from concourse.masks import make_identity
+
+K, T, S, N, H = 512, 2048, 512, 512, 512
+FLOPS = 2 * K * S * H + 2 * K * S * N + 2 * S * H * N
+
+F32 = mybir.dt.float32
+BF16 = mybir.dt.bfloat16
+I32 = mybir.dt.int32
+U32 = mybir.dt.uint32
+U16 = mybir.dt.uint16
+U8 = mybir.dt.uint8
+FP8X4 = mybir.dt.float8_e4m3fn_x4
+ALU = mybir.AluOpType
+ACT = mybir.ActivationFunctionType
+
+P = 128
+PACK = 4
+HALF = 256
+QUARTER = 128
+
+
+def tile_picked_mommax_none_po_kernel(
+    tc, x_words, x_scales, wa, wb, gt, gi, offs, two, fa, nb, out_0, out_1, out_2
+):
+    nc = tc.nc
+    with ExitStack() as ctx:
+        sb = ctx.enter_context(tc.tile_pool(name="sb", bufs=1))
+        ps = ctx.enter_context(tc.psum_pool(name="ps", bufs=1))
+
+        def tile(name, shape, dtype):
+            return sb.tile(shape, dtype, name=name, align_bytes=64)
+
+        def bank(tag, name, shape):
+            return ps.tile(shape, F32, name=name, tag=tag)
+
+        def gather(engine, out, window, offsets):
+            if engine == "vector":
+                nc.vector.tensor_copy(out, window.indirect(offsets))
+            else:
+                nc.scalar.activation(out, window.indirect(offsets), ACT.Copy)
+
+        def weave(engine, out, rows):
+            dst = out.rearrange("p (c i) t -> p c t i", i=2)
+            src = rows.rearrange("p t (c i) -> p c t i", i=2)
+            if engine == "vector":
+                nc.vector.tensor_copy(dst, src)
+            else:
+                nc.scalar.copy(dst, src)
+
+        def quantize(codes, scales, woven):
+            nc.vector.quantize_mx(out=codes.bitcast(FP8X4), scales=scales, in_=woven.rearrange("p c t -> p (c t)"))
+
+        def product(out, lhs, lhs_scale, rhs, rhs_scale):
+            nc.tensor.matmul_mx(out=out, lhsT=lhs.bitcast(FP8X4), lhsT_scale=lhs_scale, rhs=rhs.bitcast(FP8X4),
+                                rhs_scale=rhs_scale, start=True, stop=True)
+
+        offs_sb = tile("offs_sb", [P, S // 16], U16)
+        two_sb = tile("two_sb", [P, S // 16], U16)
+        fa_sb = tile("fa_sb", [P, H // 16], U16)
+        nb_sb = tile("nb_sb", [P, N // 16], U16)
+        xs = sb.tile([P, T], U8, name="xs", tag="xs_then_xq_a", align_bytes=64)
+        xw = tile("xw", [P, T], I32)
+        g_rows = tile("g_rows", [P, P], F32)
+        ident = tile("ident", [P, P], F32)
+
+        nc.vector.memset(xs[:].bitcast(I32), 0)
+        nc.gpsimd.memset(g_rows[:], 0.0)
+        make_identity(nc, ident[:])
+
+        nc.sync.dma_start(offs_sb[:], offs)
+        nc.sync.dma_start(two_sb[:], two)
+        nc.sync.dma_start(xw[:], x_words[0].rearrange("p c r -> p (c r)").bitcast(I32))
+        for q in range(4):
+            nc.scalar.dma_start(xs[32 * q : 32 * q + 4, :].bitcast(I32), x_scales[0, 4 * q : 4 * q + 4, :].bitcast(I32))
+        for v, g in enumerate((gt, gi)):
+            nc.scalar.dma_start(
+                g_rows[4 * v : 4 * v + 4, :].rearrange("t (b r) -> t b r", r=8),
+                g.rearrange("(b t r) o -> t b (r o)", t=PACK, r=8),
+            )
+        w_raw = {}
+        for name, w in (("wa", wa), ("wb", wb)):
+            for h in range(2):
+                w_raw[name, h] = tile(f"{name}_raw{h}", [P, PACK, HALF], F32)
+                nc.sync.dma_start(w_raw[name, h][:], w[:, h * HALF : (h + 1) * HALF].rearrange("(p j) c -> p j c", j=PACK))
+                if (name, h) == ("wa", 0):
+                    nc.sync.dma_start(fa_sb[:], fa)
+        nc.sync.dma_start(nb_sb[:], nb)
+
+        xq, xq_s = {}, {}
+        for name in ("a", "b"):
+            xq_s[name] = tile(f"xq_s_{name}", [P, S], U8)
+        xq["b"] = tile("xq_b", [P, S], U32)
+
+        def dealt(t):
+            return t[:].rearrange("p (t b r) -> p b t r", t=PACK, r=8)
+
+        gather("vector", dealt(xq_s["a"]), xs[:], offs_sb[:])
+        gather("vector", dealt(xq_s["b"]), xs[:], two_sb[:])
+        xq["a"] = sb.tile([P, S], U32, name="xq_a", tag="xs_then_xq_a", align_bytes=64)
+        gather("vector", dealt(xq["a"]), xw[:].bitcast(U32), offs_sb[:])
+
+        g_ps = bank("bank7", "g_ps", [P, P])
+        nc.tensor.transpose(g_ps[:], g_rows[:], ident[:])
+        gt_abs = tile("gt_abs", [P, PACK], F32)
+        gt_pos = tile("gt_pos", [P, PACK], F32)
+        gi_signed = tile("gi_signed", [P, PACK], F32)
+        nc.scalar.activation(gt_abs[:], g_ps[:, 0:PACK], ACT.Abs)
+        nc.vector.tensor_scalar(gt_pos[:], g_ps[:, 0:PACK], 0.0, 2.0, ALU.is_ge, ALU.mult)
+        nc.vector.scalar_tensor_tensor(gi_signed[:], gt_pos[:], -1.0, g_ps[:, PACK : 2 * PACK], ALU.add, ALU.mult)
+
+        gather("vector", dealt(xq["b"]), xw[:].bitcast(U32), two_sb[:])
+
+        wq, wq_s = {}, {}
+        for name in ("wa", "wb"):
+            wq[name] = tile(f"{name}_q", [P, H], U32)
+            wq_s[name] = tile(f"{name}_qs", [P, H], U8)
+
+        def quantize_weight(name, h, engine):
+            woven = tile(f"{name}_woven{h}", [P, HALF, PACK], BF16)
+            weave(engine, woven[:], w_raw[name, h][:])
+            cols = slice(h * HALF, (h + 1) * HALF)
+            quantize(wq[name][:, cols], wq_s[name][:, cols], woven[:])
+
+        a_win = [tile(f"a_win{t}", [P, H], F32) for t in range(PACK)]
+        a_got = tile("a_got", [P, PACK, H], F32)
+        z_rows = tile("z_rows", [P, PACK, H], BF16)
+        a_ps = {}
+        for h, engine in enumerate(("scalar", "vector")):
+            quantize_weight("wa", h, engine)
+            cols = slice(h * HALF, (h + 1) * HALF)
+            for pair in range(2):
+                a_ps[h, pair] = bank(f"bank{2 * h + pair}", f"a_ps{h}{pair}", [P, 2, HALF])
+                for e in range(2):
+                    rows = slice((2 * pair + e) * P, (2 * pair + e + 1) * P)
+                    product(a_ps[h, pair][:, e, :], xq["a"][:, rows], xq_s["a"][:, rows], wq["wa"][:, cols], wq_s["wa"][:, cols])
+        for h in range(2):
+            for t in range(PACK):
+                nc.scalar.activation(a_win[t][:, h * HALF : (h + 1) * HALF], a_ps[h, t // 2][:, t % 2, :], ACT.Copy, scale=gt_abs[:, t : t + 1])
+                if h == 1:
+                    for g in range(2):
+                        gather("scalar", a_got[:, t, g * HALF : (g + 1) * HALF], a_win[t][:], fa_sb[:, 16 * g : 16 * g + 16])
+
+        quantize_weight("wb", 0, "vector")
+        quantize_weight("wb", 1, "vector")
+        z2_woven = tile("z2_woven", [P, N, PACK], BF16)
+        z2q = tile("z2q", [P, N], U32)
+        z2q_s = tile("z2q_s", [P, N], U8)
+        for c in range(4):
+            cols = slice(c * QUARTER, (c + 1) * QUARTER)
+            b_ps = bank(f"bank{4 + c}", f"b_ps{c}", [P, PACK, QUARTER])
+            for t in range(PACK):
+                rows = slice(t * P, (t + 1) * P)
+                product(b_ps[:, t, :], xq["b"][:, rows], xq_s["b"][:, rows], wq["wb"][:, cols], wq_s["wb"][:, cols])
+            nc.vector.tensor_tensor(z_rows[:, c, :], a_got[:, c, :], a_win[c][:], ALU.max)
+            nc.vector.tensor_tensor(
+                z2_woven[:, cols, :], b_ps[:].rearrange("p t n -> p n t"),
+                gi_signed[:].unsqueeze(1).to_broadcast([P, QUARTER, PACK]), ALU.mult,
+            )
+            if c == 2:
+                quantize(z2q[:, 0:HALF], z2q_s[:, 0:HALF], z2_woven[:, 0:HALF, :])
+        quantize(z2q[:, HALF:N], z2q_s[:, HALF:N], z2_woven[:, HALF:N, :])
+
+        cv_win = [tile(f"cv_win{u}", [P, N], F32) for u in range(PACK)]
+        cv_got = tile("cv_got", [P, PACK, N], F32)
+        z_woven = [tile(f"z_woven{u}", [P, P, PACK], BF16) for u in range(PACK)]
+        zq = [tile(f"zq{u}", [P, P], U32) for u in range(PACK)]
+        zq_s = [tile(f"zq_s{u}", [P, P], U8) for u in range(PACK)]
+        z_by_u = z_rows[:].rearrange("p t (m u) -> p u m t", u=PACK)
+        cv_ps = []
+        for u in range(PACK):
+            if u < PACK - 1:
+                nc.scalar.copy(z_woven[u][:], z_by_u[:, u])
+            else:
+                nc.vector.tensor_copy(z_woven[u][:], z_by_u[:, u])
+        for u in range(PACK):
+            quantize(zq[u][:], zq_s[u][:], z_woven[u][:])
+            cv_ps.append(bank(f"bank{u}", f"cv_ps{u}", [P, N]))
+            product(cv_ps[u][:], zq[u][:], zq_s[u][:], z2q[:], z2q_s[:])
+
+        out_rows = out_0.rearrange("(p u) n -> p u n", u=PACK)
+        words = out_1[0].rearrange("p c r -> p (c r)").bitcast(I32)
+        oq = tile("oq", [P, N], I32)
+        oq_s = tile("oq_s", [P, N], U8)
+        chunks = ((0, 256), (256, 384), (384, 512))
+        res = [tile(f"res{i}", [P, PACK, hi - lo], F32) for i, (lo, hi) in enumerate(chunks)]
+
+        def fetch(engine, u, lo, hi):
+            gather(engine, cv_got[:, u, lo:hi], cv_win[u][:], nb_sb[:, lo // 16 : hi // 16])
+
+        def larger(i, u):
+            lo, hi = chunks[i]
+            nc.vector.tensor_tensor(res[i][:, u, :], cv_got[:, u, lo:hi], cv_win[u][:, lo:hi], ALU.max)
+
+        def hand_out(i):
+            lo, hi = chunks[i]
+            nc.sync.dma_start(out_rows[:, :, lo:hi], res[i][:])
+            woven = tile(f"out_woven{i}", [P, hi - lo, PACK], BF16)
+            weave("vector", woven[:], res[i][:])
+            quantize(oq[:, lo:hi], oq_s[:, lo:hi], woven[:])
+            nc.sync.dma_start(words[:, lo:hi], oq[:, lo:hi])
+
+        for u in range(PACK):
+            nc.scalar.activation(cv_win[u][:], cv_ps[u][:], ACT.Copy, scale=0.0625)
+            fetch("scalar", u, 0, HALF)
+            if u < 2:
+                fetch("vector", u, HALF, N)
+            larger(0, u)
+            if u < 2:
+                larger(1, u)
+                larger(2, u)
+        hand_out(0)
+        for i in (1, 2):
+            for u in (2, 3):
+                fetch("scalar", u, *chunks[i])
+                larger(i, u)
+            hand_out(i)
+        for q in range(4):
+            queue = nc.scalar if q % 2 == 0 else nc.sync
+            queue.dma_start(out_2[0, 4 * q : 4 * q + 4, :].bitcast(I32), oq_s[32 * q : 32 * q + 4, :].bitcast(I32))

@@ -1,7 +1,6 @@
 from contextlib import ExitStack
 
 import concourse.mybir as mybir
-from concourse.masks import make_identity
 
 K, T, S, N, H = 512, 2048, 512, 512, 512
 FLOPS = 2 * K * S * H + 2 * K * S * N + 2 * S * H * N
@@ -20,6 +19,7 @@ P = 128
 PACK = 4
 HALF = 256
 QUARTER = 128
+ON_VECTOR = 1
 
 
 def tile_picked_mommax_none_po_kernel(
@@ -28,6 +28,7 @@ def tile_picked_mommax_none_po_kernel(
     nc = tc.nc
     with ExitStack() as ctx:
         sb = ctx.enter_context(tc.tile_pool(name="sb", bufs=1))
+        shared = ctx.enter_context(tc.tile_pool(name="shared", bufs=1))
         ps = ctx.enter_context(tc.psum_pool(name="ps", bufs=1))
 
         def tile(name, shape, dtype):
@@ -62,32 +63,33 @@ def tile_picked_mommax_none_po_kernel(
         fa_sb = tile("fa_sb", [P, H // 16], U16)
         nb_sb = tile("nb_sb", [P, N // 16], U16)
         xs = sb.tile([P, T], U8, name="xs", tag="xs_then_xq_a", align_bytes=64)
-        xw = tile("xw", [P, T], I32)
         g_rows = tile("g_rows", [P, P], F32)
         ident = tile("ident", [P, P], F32)
 
-        nc.vector.memset(xs[:].bitcast(I32), 0)
+        nc.gpsimd.memset(xs[:].bitcast(I32), 0)
+        zeros = shared.tile([P, P], F32, name="zeros", offset=4 * T - 2 * P)
+        nc.gpsimd.memset(zeros[:], 0.0)
+        nc.gpsimd.affine_select(out=ident[:], in_=zeros[:], compare_op=ALU.not_equal, fill=1.0, base=0, pattern=[[-1, P]], channel_multiplier=1)
         nc.gpsimd.memset(g_rows[:], 0.0)
-        make_identity(nc, ident[:])
 
-        nc.sync.dma_start(offs_sb[:], offs)
-        nc.sync.dma_start(two_sb[:], two)
-        nc.sync.dma_start(xw[:], x_words[0].rearrange("p c r -> p (c r)").bitcast(I32))
+        xw = shared.tile([P, T], I32, name="xw", offset=0)
+        wa_raw = sb.tile([P, PACK, H], F32, name="wa_raw", tag="wa_then_wb1")
+        w_raw = {("wa", h): wa_raw[:, :, h * HALF : (h + 1) * HALF] for h in range(2)}
+        wb_raw0 = shared.tile([P, PACK, HALF], F32, name="wb_raw0", offset=4 * T)
+        w_raw["wb", 0] = wb_raw0[:]
+
+        for list_sb, list_in in ((offs_sb, offs), (two_sb, two), (fa_sb, fa), (nb_sb, nb)):
+            nc.sync.dma_start(list_sb[:], list_in)
+        nc.sync.dma_start(wa_raw[:], wa.rearrange("(p j) c -> p j c", j=PACK))
         for q in range(4):
             nc.scalar.dma_start(xs[32 * q : 32 * q + 4, :].bitcast(I32), x_scales[0, 4 * q : 4 * q + 4, :].bitcast(I32))
+        nc.sync.dma_start(xw[:], x_words[0].rearrange("p c r -> p (c r)").bitcast(I32))
         for v, g in enumerate((gt, gi)):
-            nc.scalar.dma_start(
+            nc.sync.dma_start(
                 g_rows[4 * v : 4 * v + 4, :].rearrange("t (b r) -> t b r", r=8),
                 g.rearrange("(b t r) o -> t b (r o)", t=PACK, r=8),
             )
-        w_raw = {}
-        for name, w in (("wa", wa), ("wb", wb)):
-            for h in range(2):
-                w_raw[name, h] = tile(f"{name}_raw{h}", [P, PACK, HALF], F32)
-                nc.sync.dma_start(w_raw[name, h][:], w[:, h * HALF : (h + 1) * HALF].rearrange("(p j) c -> p j c", j=PACK))
-                if (name, h) == ("wa", 0):
-                    nc.sync.dma_start(fa_sb[:], fa)
-        nc.sync.dma_start(nb_sb[:], nb)
+        nc.sync.dma_start(wb_raw0[:], wb[:, 0:HALF].rearrange("(p j) c -> p j c", j=PACK))
 
         xq, xq_s = {}, {}
         for name in ("a", "b"):
@@ -99,19 +101,9 @@ def tile_picked_mommax_none_po_kernel(
 
         gather("vector", dealt(xq_s["a"]), xs[:], offs_sb[:])
         gather("vector", dealt(xq_s["b"]), xs[:], two_sb[:])
-        xq["a"] = sb.tile([P, S], U32, name="xq_a", tag="xs_then_xq_a", align_bytes=64)
-        gather("vector", dealt(xq["a"]), xw[:].bitcast(U32), offs_sb[:])
 
         g_ps = bank("bank7", "g_ps", [P, P])
         nc.tensor.transpose(g_ps[:], g_rows[:], ident[:])
-        gt_abs = tile("gt_abs", [P, PACK], F32)
-        gt_pos = tile("gt_pos", [P, PACK], F32)
-        gi_signed = tile("gi_signed", [P, PACK], F32)
-        nc.scalar.activation(gt_abs[:], g_ps[:, 0:PACK], ACT.Abs)
-        nc.vector.tensor_scalar(gt_pos[:], g_ps[:, 0:PACK], 0.0, 2.0, ALU.is_ge, ALU.mult)
-        nc.vector.scalar_tensor_tensor(gi_signed[:], gt_pos[:], -1.0, g_ps[:, PACK : 2 * PACK], ALU.add, ALU.mult)
-
-        gather("vector", dealt(xq["b"]), xw[:].bitcast(U32), two_sb[:])
 
         wq, wq_s = {}, {}
         for name in ("wa", "wb"):
@@ -119,49 +111,63 @@ def tile_picked_mommax_none_po_kernel(
             wq_s[name] = tile(f"{name}_qs", [P, H], U8)
 
         def quantize_weight(name, h, engine):
-            woven = tile(f"{name}_woven{h}", [P, HALF, PACK], BF16)
-            weave(engine, woven[:], w_raw[name, h][:])
+            woven = sb.tile([P, HALF, PACK], BF16, name=f"{name}_woven{h}", tag=f"{name}_woven{h}", align_bytes=64)
             cols = slice(h * HALF, (h + 1) * HALF)
+            weave(engine, woven[:], w_raw[name, h])
             quantize(wq[name][:, cols], wq_s[name][:, cols], woven[:])
+
+        quantize_weight("wa", 0, "scalar")
+        quantize_weight("wa", 1, "scalar")
+        wb_raw1 = sb.tile([P, PACK, HALF], F32, name="wb_raw1", tag="wa_then_wb1")
+        w_raw["wb", 1] = wb_raw1[:]
+        nc.sync.dma_start(wb_raw1[:], wb[:, HALF:N].rearrange("(p j) c -> p j c", j=PACK))
+        xq["a"] = sb.tile([P, S], U32, name="xq_a", tag="xs_then_xq_a", align_bytes=64)
+        gather("vector", dealt(xq["a"]), xw[:].bitcast(U32), offs_sb[:])
+        gather("vector", dealt(xq["b"]), xw[:].bitcast(U32), two_sb[:])
+
+        quantize_weight("wb", 0, "scalar")
+        gt_abs = shared.tile([P, PACK], F32, name="gt_abs", offset=4 * T + 4 * P)
+        nc.scalar.activation(gt_abs[:], g_ps[:, 0:PACK], ACT.Abs)
 
         a_win = [tile(f"a_win{t}", [P, H], F32) for t in range(PACK)]
         a_got = tile("a_got", [P, PACK, H], F32)
         z_rows = tile("z_rows", [P, PACK, H], BF16)
-        a_ps = {}
-        for h, engine in enumerate(("scalar", "vector")):
-            quantize_weight("wa", h, engine)
-            cols = slice(h * HALF, (h + 1) * HALF)
-            for pair in range(2):
-                a_ps[h, pair] = bank(f"bank{2 * h + pair}", f"a_ps{h}{pair}", [P, 2, HALF])
-                for e in range(2):
-                    rows = slice((2 * pair + e) * P, (2 * pair + e + 1) * P)
-                    product(a_ps[h, pair][:, e, :], xq["a"][:, rows], xq_s["a"][:, rows], wq["wa"][:, cols], wq_s["wa"][:, cols])
-        for h in range(2):
-            for t in range(PACK):
-                nc.scalar.activation(a_win[t][:, h * HALF : (h + 1) * HALF], a_ps[h, t // 2][:, t % 2, :], ACT.Copy, scale=gt_abs[:, t : t + 1])
-                if h == 1:
-                    for g in range(2):
-                        gather("scalar", a_got[:, t, g * HALF : (g + 1) * HALF], a_win[t][:], fa_sb[:, 16 * g : 16 * g + 16])
+        for t in range(PACK):
+            a_ps = bank(f"bank{t}", f"a_ps{t}", [P, H])
+            rows = slice(t * P, (t + 1) * P)
+            product(a_ps[:], xq["a"][:, rows], xq_s["a"][:, rows], wq["wa"][:], wq_s["wa"][:])
+            nc.scalar.activation(a_win[t][:], a_ps[:], ACT.Copy, scale=gt_abs[:, t : t + 1])
+            for g in range(2):
+                gather("scalar", a_got[:, t, g * HALF : (g + 1) * HALF], a_win[t][:], fa_sb[:, 16 * g : 16 * g + 16])
 
-        quantize_weight("wb", 0, "vector")
+        gt_pos = sb.tile([P, PACK], F32, name="gt_pos", tag="wb_woven0", align_bytes=64)
+        gi_signed = tile("gi_signed", [P, PACK], F32)
+        nc.vector.tensor_scalar(gt_pos[:], g_ps[:, 0:PACK], 0.0, 2.0, ALU.is_ge, ALU.mult)
+        nc.vector.scalar_tensor_tensor(gi_signed[:], gt_pos[:], -1.0, g_ps[:, PACK : 2 * PACK], ALU.add, ALU.mult)
         quantize_weight("wb", 1, "vector")
         z2_woven = tile("z2_woven", [P, N, PACK], BF16)
         z2q = tile("z2q", [P, N], U32)
         z2q_s = tile("z2q_s", [P, N], U8)
+
+        def larger_a(t):
+            nc.vector.tensor_tensor(z_rows[:, t, :], a_got[:, t, :], a_win[t][:], ALU.max)
+
         for c in range(4):
             cols = slice(c * QUARTER, (c + 1) * QUARTER)
             b_ps = bank(f"bank{4 + c}", f"b_ps{c}", [P, PACK, QUARTER])
             for t in range(PACK):
                 rows = slice(t * P, (t + 1) * P)
                 product(b_ps[:, t, :], xq["b"][:, rows], xq_s["b"][:, rows], wq["wb"][:, cols], wq_s["wb"][:, cols])
-            nc.vector.tensor_tensor(z_rows[:, c, :], a_got[:, c, :], a_win[c][:], ALU.max)
             nc.vector.tensor_tensor(
                 z2_woven[:, cols, :], b_ps[:].rearrange("p t n -> p n t"),
                 gi_signed[:].unsqueeze(1).to_broadcast([P, QUARTER, PACK]), ALU.mult,
             )
             if c == 2:
                 quantize(z2q[:, 0:HALF], z2q_s[:, 0:HALF], z2_woven[:, 0:HALF, :])
+            else:
+                larger_a(min(c, 2))
         quantize(z2q[:, HALF:N], z2q_s[:, HALF:N], z2_woven[:, HALF:N, :])
+        larger_a(3)
 
         cv_win = [tile(f"cv_win{u}", [P, N], F32) for u in range(PACK)]
         cv_got = tile("cv_got", [P, PACK, N], F32)
@@ -171,7 +177,7 @@ def tile_picked_mommax_none_po_kernel(
         z_by_u = z_rows[:].rearrange("p t (m u) -> p u m t", u=PACK)
         cv_ps = []
         for u in range(PACK):
-            if u < PACK - 1:
+            if u in (1, 2):
                 nc.scalar.copy(z_woven[u][:], z_by_u[:, u])
             else:
                 nc.vector.tensor_copy(z_woven[u][:], z_by_u[:, u])
@@ -184,39 +190,35 @@ def tile_picked_mommax_none_po_kernel(
         words = out_1[0].rearrange("p c r -> p (c r)").bitcast(I32)
         oq = tile("oq", [P, N], I32)
         oq_s = tile("oq_s", [P, N], U8)
-        chunks = ((0, 256), (256, 384), (384, 512))
-        res = [tile(f"res{i}", [P, PACK, hi - lo], F32) for i, (lo, hi) in enumerate(chunks)]
+        res = tile("res", [P, PACK, N], F32)
 
         def fetch(engine, u, lo, hi):
             gather(engine, cv_got[:, u, lo:hi], cv_win[u][:], nb_sb[:, lo // 16 : hi // 16])
 
-        def larger(i, u):
-            lo, hi = chunks[i]
-            nc.vector.tensor_tensor(res[i][:, u, :], cv_got[:, u, lo:hi], cv_win[u][:, lo:hi], ALU.max)
+        def larger_cv(u, lo, hi):
+            nc.vector.tensor_tensor(res[:, u, lo:hi], cv_got[:, u, lo:hi], cv_win[u][:, lo:hi], ALU.max)
 
-        def hand_out(i):
-            lo, hi = chunks[i]
-            nc.sync.dma_start(out_rows[:, :, lo:hi], res[i][:])
-            woven = tile(f"out_woven{i}", [P, hi - lo, PACK], BF16)
-            weave("vector", woven[:], res[i][:])
+        def hand_out(lo, hi):
+            nc.sync.dma_start(out_rows[:, :, lo:hi], res[:, :, lo:hi])
+            woven = tile(f"out_woven{lo}", [P, hi - lo, PACK], BF16)
+            weave("vector", woven[:], res[:, :, lo:hi])
             quantize(oq[:, lo:hi], oq_s[:, lo:hi], woven[:])
             nc.sync.dma_start(words[:, lo:hi], oq[:, lo:hi])
 
         for u in range(PACK):
             nc.scalar.activation(cv_win[u][:], cv_ps[u][:], ACT.Copy, scale=0.0625)
             fetch("scalar", u, 0, HALF)
-            if u < 2:
+            if u < ON_VECTOR:
                 fetch("vector", u, HALF, N)
-            larger(0, u)
-            if u < 2:
-                larger(1, u)
-                larger(2, u)
-        hand_out(0)
-        for i in (1, 2):
-            for u in (2, 3):
-                fetch("scalar", u, *chunks[i])
-                larger(i, u)
-            hand_out(i)
+                larger_cv(u, 0, N)
+            else:
+                larger_cv(u, 0, HALF)
+        hand_out(0, HALF)
+        for lo, hi in ((HALF, HALF + QUARTER), (HALF + QUARTER, N)):
+            for u in range(ON_VECTOR, PACK):
+                fetch("scalar", u, lo, hi)
+                larger_cv(u, lo, hi)
+            hand_out(lo, hi)
         for q in range(4):
             queue = nc.scalar if q % 2 == 0 else nc.sync
             queue.dma_start(out_2[0, 4 * q : 4 * q + 4, :].bitcast(I32), oq_s[32 * q : 32 * q + 4, :].bitcast(I32))

@@ -19,7 +19,11 @@ P = 128
 PACK = 4
 HALF = 256
 QUARTER = 128
-ON_VECTOR = 1
+WB0_AT = 4 * T
+XQ_A_AT = WB0_AT + 4 * PACK * HALF
+XS_AT = XQ_A_AT + 3 * S
+G_AT = XQ_A_AT + 4 * S
+XQ_B_AT = G_AT + 64
 
 
 def tile_picked_mommax_none_po_kernel(
@@ -33,6 +37,9 @@ def tile_picked_mommax_none_po_kernel(
 
         def tile(name, shape, dtype):
             return sb.tile(shape, dtype, name=name, align_bytes=64)
+
+        def placed(name, shape, dtype, offset):
+            return shared.tile(shape, dtype, name=name, offset=offset, align_bytes=64)
 
         def bank(tag, name, shape):
             return ps.tile(shape, F32, name=name, tag=tag)
@@ -58,52 +65,51 @@ def tile_picked_mommax_none_po_kernel(
             nc.tensor.matmul_mx(out=out, lhsT=lhs.bitcast(FP8X4), lhsT_scale=lhs_scale, rhs=rhs.bitcast(FP8X4),
                                 rhs_scale=rhs_scale, start=True, stop=True)
 
+        def load_place_weights(rows, g):
+            nc.sync.dma_start(
+                rows[0:PACK, :].rearrange("t (b r) -> t b r", r=8), g.rearrange("(b t r) o -> t b (r o)", t=PACK, r=8)
+            )
+
         offs_sb = tile("offs_sb", [P, S // 16], U16)
         two_sb = tile("two_sb", [P, S // 16], U16)
         fa_sb = tile("fa_sb", [P, H // 16], U16)
         nb_sb = tile("nb_sb", [P, N // 16], U16)
-        xs = sb.tile([P, T], U8, name="xs", tag="xs_then_xq_a", align_bytes=64)
-        g_rows = tile("g_rows", [P, P], F32)
+        xs = placed("xs", [P, T], U8, XS_AT)
+        gt_rows = tile("gt_rows", [P, P], F32)
         ident = tile("ident", [P, P], F32)
 
         nc.gpsimd.memset(xs[:].bitcast(I32), 0)
-        zeros = shared.tile([P, P], F32, name="zeros", offset=4 * T - 2 * P)
+        zeros = placed("zeros", [P, P], F32, WB0_AT - 2 * P)
         nc.gpsimd.memset(zeros[:], 0.0)
         nc.gpsimd.affine_select(out=ident[:], in_=zeros[:], compare_op=ALU.not_equal, fill=1.0, base=0, pattern=[[-1, P]], channel_multiplier=1)
-        nc.gpsimd.memset(g_rows[:], 0.0)
+        nc.gpsimd.memset(gt_rows[:], 0.0)
 
-        xw = shared.tile([P, T], I32, name="xw", offset=0)
-        wa_raw = sb.tile([P, PACK, H], F32, name="wa_raw", tag="wa_then_wb1")
-        w_raw = {("wa", h): wa_raw[:, :, h * HALF : (h + 1) * HALF] for h in range(2)}
-        wb_raw0 = shared.tile([P, PACK, HALF], F32, name="wb_raw0", offset=4 * T)
+        xw = placed("xw", [P, T], I32, 0)
+        wa_raw0 = sb.tile([P, PACK, HALF], F32, name="wa_raw0", tag="wa0_then_gi_rows")
+        wa_raw1 = sb.tile([P, PACK, HALF], F32, name="wa_raw1", tag="wa1_then_wb1")
+        w_raw = {("wa", 0): wa_raw0[:], ("wa", 1): wa_raw1[:]}
+        wb_raw0 = placed("wb_raw0", [P, PACK, HALF], F32, WB0_AT)
         w_raw["wb", 0] = wb_raw0[:]
 
         for list_sb, list_in in ((offs_sb, offs), (two_sb, two), (fa_sb, fa), (nb_sb, nb)):
             nc.sync.dma_start(list_sb[:], list_in)
-        nc.sync.dma_start(wa_raw[:], wa.rearrange("(p j) c -> p j c", j=PACK))
+        for h in range(2):
+            nc.sync.dma_start(w_raw["wa", h], wa[:, h * HALF : (h + 1) * HALF].rearrange("(p j) c -> p j c", j=PACK))
         for q in range(4):
             nc.scalar.dma_start(xs[32 * q : 32 * q + 4, :].bitcast(I32), x_scales[0, 4 * q : 4 * q + 4, :].bitcast(I32))
         nc.sync.dma_start(xw[:], x_words[0].rearrange("p c r -> p (c r)").bitcast(I32))
-        for v, g in enumerate((gt, gi)):
-            nc.sync.dma_start(
-                g_rows[4 * v : 4 * v + 4, :].rearrange("t (b r) -> t b r", r=8),
-                g.rearrange("(b t r) o -> t b (r o)", t=PACK, r=8),
-            )
+        load_place_weights(gt_rows, gt)
         nc.sync.dma_start(wb_raw0[:], wb[:, 0:HALF].rearrange("(p j) c -> p j c", j=PACK))
 
         xq, xq_s = {}, {}
         for name in ("a", "b"):
             xq_s[name] = tile(f"xq_s_{name}", [P, S], U8)
-        xq["b"] = tile("xq_b", [P, S], U32)
 
         def dealt(t):
             return t[:].rearrange("p (t b r) -> p b t r", t=PACK, r=8)
 
         gather("vector", dealt(xq_s["a"]), xs[:], offs_sb[:])
         gather("vector", dealt(xq_s["b"]), xs[:], two_sb[:])
-
-        g_ps = bank("bank7", "g_ps", [P, P])
-        nc.tensor.transpose(g_ps[:], g_rows[:], ident[:])
 
         wq, wq_s = {}, {}
         for name in ("wa", "wb"):
@@ -117,18 +123,28 @@ def tile_picked_mommax_none_po_kernel(
             quantize(wq[name][:, cols], wq_s[name][:, cols], woven[:])
 
         quantize_weight("wa", 0, "scalar")
+        gi_rows = sb.tile([P, P], F32, name="gi_rows", tag="wa0_then_gi_rows")
+        nc.gpsimd.memset(gi_rows[:], 0.0)
+        load_place_weights(gi_rows, gi)
         quantize_weight("wa", 1, "scalar")
-        wb_raw1 = sb.tile([P, PACK, HALF], F32, name="wb_raw1", tag="wa_then_wb1")
+        wb_raw1 = sb.tile([P, PACK, HALF], F32, name="wb_raw1", tag="wa1_then_wb1")
         w_raw["wb", 1] = wb_raw1[:]
         nc.sync.dma_start(wb_raw1[:], wb[:, HALF:N].rearrange("(p j) c -> p j c", j=PACK))
-        xq["a"] = sb.tile([P, S], U32, name="xq_a", tag="xs_then_xq_a", align_bytes=64)
+        xq["a"] = placed("xq_a", [P, S], U32, XQ_A_AT)
+        xq["b"] = placed("xq_b", [P, S], U32, XQ_B_AT)
         gather("vector", dealt(xq["a"]), xw[:].bitcast(U32), offs_sb[:])
+        gt_ps = bank("bank0", "gt_ps", [P, P])
+        nc.tensor.transpose(gt_ps[:], gt_rows[:], ident[:])
+        gt_sb = placed("gt_sb", [P, PACK], F32, G_AT)
+        nc.vector.tensor_copy(gt_sb[:], gt_ps[:, 0:PACK])
         gather("vector", dealt(xq["b"]), xw[:].bitcast(U32), two_sb[:])
+        gt_pos = tile("gt_pos", [P, PACK], F32)
+        nc.vector.tensor_scalar(gt_pos[:], gt_sb[:], 0.0, 2.0, ALU.is_ge, ALU.mult)
 
         quantize_weight("wb", 0, "scalar")
-        gt_abs = shared.tile([P, PACK], F32, name="gt_abs", offset=4 * T + 4 * P)
-        nc.scalar.activation(gt_abs[:], g_ps[:, 0:PACK], ACT.Abs)
 
+        gt_abs = placed("gt_abs", [P, PACK], F32, WB0_AT + 4 * P)
+        nc.scalar.activation(gt_abs[:], gt_sb[:], ACT.Abs)
         a_win = [tile(f"a_win{t}", [P, H], F32) for t in range(PACK)]
         a_got = tile("a_got", [P, PACK, H], F32)
         z_rows = tile("z_rows", [P, PACK, H], BF16)
@@ -140,17 +156,17 @@ def tile_picked_mommax_none_po_kernel(
             for g in range(2):
                 gather("scalar", a_got[:, t, g * HALF : (g + 1) * HALF], a_win[t][:], fa_sb[:, 16 * g : 16 * g + 16])
 
-        gt_pos = sb.tile([P, PACK], F32, name="gt_pos", tag="wb_woven0", align_bytes=64)
-        gi_signed = tile("gi_signed", [P, PACK], F32)
-        nc.vector.tensor_scalar(gt_pos[:], g_ps[:, 0:PACK], 0.0, 2.0, ALU.is_ge, ALU.mult)
-        nc.vector.scalar_tensor_tensor(gi_signed[:], gt_pos[:], -1.0, g_ps[:, PACK : 2 * PACK], ALU.add, ALU.mult)
         quantize_weight("wb", 1, "vector")
+        gi_ps = bank("bank0", "gi_ps", [P, P])
+        nc.tensor.transpose(gi_ps[:], gi_rows[:], ident[:])
+        gi_signed = tile("gi_signed", [P, PACK], F32)
+        nc.vector.scalar_tensor_tensor(gi_signed[:], gt_pos[:], -1.0, gi_ps[:, 0:PACK], ALU.add, ALU.mult)
         z2_woven = tile("z2_woven", [P, N, PACK], BF16)
         z2q = tile("z2q", [P, N], U32)
         z2q_s = tile("z2q_s", [P, N], U8)
 
-        def larger_a(t):
-            nc.vector.tensor_tensor(z_rows[:, t, :], a_got[:, t, :], a_win[t][:], ALU.max)
+        def larger_a(t, lo=0, hi=H):
+            nc.vector.tensor_tensor(z_rows[:, t, lo:hi], a_got[:, t, lo:hi], a_win[t][:, lo:hi], ALU.max)
 
         for c in range(4):
             cols = slice(c * QUARTER, (c + 1) * QUARTER)
@@ -167,7 +183,8 @@ def tile_picked_mommax_none_po_kernel(
             else:
                 larger_a(min(c, 2))
         quantize(z2q[:, HALF:N], z2q_s[:, HALF:N], z2_woven[:, HALF:N, :])
-        larger_a(3)
+        larger_a(3, 0, HALF)
+        larger_a(3, HALF, H)
 
         cv_win = [tile(f"cv_win{u}", [P, N], F32) for u in range(PACK)]
         cv_got = tile("cv_got", [P, PACK, N], F32)
@@ -198,27 +215,30 @@ def tile_picked_mommax_none_po_kernel(
         def larger_cv(u, lo, hi):
             nc.vector.tensor_tensor(res[:, u, lo:hi], cv_got[:, u, lo:hi], cv_win[u][:, lo:hi], ALU.max)
 
-        def hand_out(lo, hi):
+        def hand_out(lo, hi, engine):
             nc.sync.dma_start(out_rows[:, :, lo:hi], res[:, :, lo:hi])
             woven = tile(f"out_woven{lo}", [P, hi - lo, PACK], BF16)
-            weave("vector", woven[:], res[:, :, lo:hi])
+            weave(engine, woven[:], res[:, :, lo:hi])
             quantize(oq[:, lo:hi], oq_s[:, lo:hi], woven[:])
             nc.sync.dma_start(words[:, lo:hi], oq[:, lo:hi])
 
         for u in range(PACK):
-            nc.scalar.activation(cv_win[u][:], cv_ps[u][:], ACT.Copy, scale=0.0625)
-            fetch("scalar", u, 0, HALF)
-            if u < ON_VECTOR:
-                fetch("vector", u, HALF, N)
-                larger_cv(u, 0, N)
+            if u % 2 == 0:
+                nc.scalar.activation(cv_win[u][:], cv_ps[u][:], ACT.Copy, scale=0.0625)
             else:
-                larger_cv(u, 0, HALF)
-        hand_out(0, HALF)
-        for lo, hi in ((HALF, HALF + QUARTER), (HALF + QUARTER, N)):
-            for u in range(ON_VECTOR, PACK):
+                nc.vector.tensor_scalar(cv_win[u][:], cv_ps[u][:], 0.0625, None, ALU.mult)
+        for u in range(PACK):
+            fetch("scalar", u, 0, HALF)
+            larger_cv(u, 0, HALF)
+        hand_out(0, HALF, "vector")
+        for u in (0, 1):
+            fetch("vector" if u == 0 else "scalar", u, HALF, N)
+            larger_cv(u, HALF, N)
+        for lo, hi, engine in ((HALF, HALF + QUARTER, "scalar"), (HALF + QUARTER, N, "vector")):
+            for u in (2, 3):
                 fetch("scalar", u, lo, hi)
                 larger_cv(u, lo, hi)
-            hand_out(lo, hi)
+            hand_out(lo, hi, engine)
         for q in range(4):
             queue = nc.scalar if q % 2 == 0 else nc.sync
             queue.dma_start(out_2[0, 4 * q : 4 * q + 4, :].bitcast(I32), oq_s[32 * q : 32 * q + 4, :].bitcast(I32))

from contextlib import ExitStack

import concourse.mybir as mybir

K, T, S, N, H = 512, 2048, 512, 512, 512
FLOPS = 2 * K * S * H + 2 * K * S * N + 2 * S * H * N

F32 = mybir.dt.float32
BF16 = mybir.dt.bfloat16
I32 = mybir.dt.int32
U32 = mybir.dt.uint32
U16 = mybir.dt.uint16
U8 = mybir.dt.uint8
FP8X4 = mybir.dt.float8_e4m3fn_x4
ALU = mybir.AluOpType
ACT = mybir.ActivationFunctionType

P = 128
PACK = 4
HALF = 256
QUARTER = 128
WB0_AT = 4 * T
XQ_A_AT = WB0_AT + 4 * PACK * HALF
XS_AT = XQ_A_AT + 3 * S
G_AT = XQ_A_AT + 4 * S
XQ_B_AT = G_AT + 64


def tile_picked_mommax_none_po_kernel(
    tc, x_words, x_scales, wa, wb, gt, gi, offs, two, fa, nb, out_0, out_1, out_2
):
    nc = tc.nc
    with ExitStack() as ctx:
        sb = ctx.enter_context(tc.tile_pool(name="sb", bufs=1))
        shared = ctx.enter_context(tc.tile_pool(name="shared", bufs=1))
        ps = ctx.enter_context(tc.psum_pool(name="ps", bufs=1))

        def tile(name, shape, dtype):
            return sb.tile(shape, dtype, name=name, align_bytes=64)

        def placed(name, shape, dtype, offset):
            return shared.tile(shape, dtype, name=name, offset=offset, align_bytes=64)

        def bank(tag, name, shape):
            return ps.tile(shape, F32, name=name, tag=tag)

        def gather(engine, out, window, offsets):
            if engine == "vector":
                nc.vector.tensor_copy(out, window.indirect(offsets))
            else:
                nc.scalar.activation(out, window.indirect(offsets), ACT.Copy)

        def weave(engine, out, rows):
            dst = out.rearrange("p (c i) t -> p c t i", i=2)
            src = rows.rearrange("p t (c i) -> p c t i", i=2)
            if engine == "vector":
                nc.vector.tensor_copy(dst, src)
            else:
                nc.scalar.copy(dst, src)

        def quantize(codes, scales, woven):
            nc.vector.quantize_mx(out=codes.bitcast(FP8X4), scales=scales, in_=woven.rearrange("p c t -> p (c t)"))

        def product(out, lhs, lhs_scale, rhs, rhs_scale):
            nc.tensor.matmul_mx(out=out, lhsT=lhs.bitcast(FP8X4), lhsT_scale=lhs_scale, rhs=rhs.bitcast(FP8X4),
                                rhs_scale=rhs_scale, start=True, stop=True)

        def load_place_weights(rows, g):
            nc.sync.dma_start(
                rows[0:PACK, :].rearrange("t (b r) -> t b r", r=8), g.rearrange("(b t r) o -> t b (r o)", t=PACK, r=8)
            )

        offs_sb = tile("offs_sb", [P, S // 16], U16)
        two_sb = tile("two_sb", [P, S // 16], U16)
        fa_sb = tile("fa_sb", [P, H // 16], U16)
        nb_sb = tile("nb_sb", [P, N // 16], U16)
        xs = placed("xs", [P, T], U8, XS_AT)
        gt_rows = tile("gt_rows", [P, P], F32)
        ident = tile("ident", [P, P], F32)

        nc.gpsimd.memset(xs[:].bitcast(I32), 0)
        zeros = placed("zeros", [P, P], F32, WB0_AT - 2 * P)
        nc.gpsimd.memset(zeros[:], 0.0)
        nc.gpsimd.affine_select(out=ident[:], in_=zeros[:], compare_op=ALU.not_equal, fill=1.0, base=0, pattern=[[-1, P]], channel_multiplier=1)
        nc.gpsimd.memset(gt_rows[:], 0.0)

        xw = placed("xw", [P, T], I32, 0)
        wa_raw0 = sb.tile([P, PACK, HALF], F32, name="wa_raw0", tag="wa0_then_gi_rows")
        wa_raw1 = sb.tile([P, PACK, HALF], F32, name="wa_raw1", tag="wa1_then_wb1")
        w_raw = {("wa", 0): wa_raw0[:], ("wa", 1): wa_raw1[:]}
        wb_raw0 = placed("wb_raw0", [P, PACK, HALF], F32, WB0_AT)
        w_raw["wb", 0] = wb_raw0[:]

        for list_sb, list_in in ((offs_sb, offs), (two_sb, two), (fa_sb, fa), (nb_sb, nb)):
            nc.sync.dma_start(list_sb[:], list_in)
        for h in range(2):
            nc.sync.dma_start(w_raw["wa", h], wa[:, h * HALF : (h + 1) * HALF].rearrange("(p j) c -> p j c", j=PACK))
        for q in range(4):
            nc.scalar.dma_start(xs[32 * q : 32 * q + 4, :].bitcast(I32), x_scales[0, 4 * q : 4 * q + 4, :].bitcast(I32))
        nc.sync.dma_start(xw[:], x_words[0].rearrange("p c r -> p (c r)").bitcast(I32))
        load_place_weights(gt_rows, gt)
        nc.sync.dma_start(wb_raw0[:], wb[:, 0:HALF].rearrange("(p j) c -> p j c", j=PACK))

        xq, xq_s = {}, {}
        for name in ("a", "b"):
            xq_s[name] = tile(f"xq_s_{name}", [P, S], U8)

        def dealt(t):
            return t[:].rearrange("p (t b r) -> p b t r", t=PACK, r=8)

        gather("vector", dealt(xq_s["a"]), xs[:], offs_sb[:])
        gather("vector", dealt(xq_s["b"]), xs[:], two_sb[:])

        wq, wq_s = {}, {}
        for name in ("wa", "wb"):
            wq[name] = tile(f"{name}_q", [P, H], U32)
            wq_s[name] = tile(f"{name}_qs", [P, H], U8)

        def quantize_weight(name, h, engine):
            woven = sb.tile([P, HALF, PACK], BF16, name=f"{name}_woven{h}", tag=f"{name}_woven{h}", align_bytes=64)
            cols = slice(h * HALF, (h + 1) * HALF)
            weave(engine, woven[:], w_raw[name, h])
            quantize(wq[name][:, cols], wq_s[name][:, cols], woven[:])

        quantize_weight("wa", 0, "scalar")
        gi_rows = sb.tile([P, P], F32, name="gi_rows", tag="wa0_then_gi_rows")
        nc.gpsimd.memset(gi_rows[:], 0.0)
        load_place_weights(gi_rows, gi)
        quantize_weight("wa", 1, "scalar")
        wb_raw1 = sb.tile([P, PACK, HALF], F32, name="wb_raw1", tag="wa1_then_wb1")
        w_raw["wb", 1] = wb_raw1[:]
        nc.sync.dma_start(wb_raw1[:], wb[:, HALF:N].rearrange("(p j) c -> p j c", j=PACK))
        xq["a"] = placed("xq_a", [P, S], U32, XQ_A_AT)
        xq["b"] = placed("xq_b", [P, S], U32, XQ_B_AT)
        gather("vector", dealt(xq["a"]), xw[:].bitcast(U32), offs_sb[:])
        gt_ps = bank("bank0", "gt_ps", [P, P])
        nc.tensor.transpose(gt_ps[:], gt_rows[:], ident[:])
        gt_sb = placed("gt_sb", [P, PACK], F32, G_AT)
        nc.vector.tensor_copy(gt_sb[:], gt_ps[:, 0:PACK])
        gather("vector", dealt(xq["b"]), xw[:].bitcast(U32), two_sb[:])
        gt_pos = tile("gt_pos", [P, PACK], F32)
        nc.vector.tensor_scalar(gt_pos[:], gt_sb[:], 0.0, 2.0, ALU.is_ge, ALU.mult)

        quantize_weight("wb", 0, "scalar")

        gt_abs = placed("gt_abs", [P, PACK], F32, WB0_AT + 4 * P)
        nc.scalar.activation(gt_abs[:], gt_sb[:], ACT.Abs)
        a_win = [tile(f"a_win{t}", [P, H], F32) for t in range(PACK)]
        a_got = tile("a_got", [P, PACK, H], F32)
        z_rows = tile("z_rows", [P, PACK, H], BF16)
        for t in range(PACK):
            a_ps = bank(f"bank{t}", f"a_ps{t}", [P, H])
            rows = slice(t * P, (t + 1) * P)
            product(a_ps[:], xq["a"][:, rows], xq_s["a"][:, rows], wq["wa"][:], wq_s["wa"][:])
            nc.scalar.activation(a_win[t][:], a_ps[:], ACT.Copy, scale=gt_abs[:, t : t + 1])
            for g in range(2):
                gather("scalar", a_got[:, t, g * HALF : (g + 1) * HALF], a_win[t][:], fa_sb[:, 16 * g : 16 * g + 16])

        quantize_weight("wb", 1, "vector")
        gi_ps = bank("bank0", "gi_ps", [P, P])
        nc.tensor.transpose(gi_ps[:], gi_rows[:], ident[:])
        gi_signed = tile("gi_signed", [P, PACK], F32)
        nc.vector.scalar_tensor_tensor(gi_signed[:], gt_pos[:], -1.0, gi_ps[:, 0:PACK], ALU.add, ALU.mult)
        z2_woven = tile("z2_woven", [P, N, PACK], BF16)
        z2q = tile("z2q", [P, N], U32)
        z2q_s = tile("z2q_s", [P, N], U8)

        def larger_a(t, lo=0, hi=H):
            nc.vector.tensor_tensor(z_rows[:, t, lo:hi], a_got[:, t, lo:hi], a_win[t][:, lo:hi], ALU.max)

        for c in range(4):
            cols = slice(c * QUARTER, (c + 1) * QUARTER)
            b_ps = bank(f"bank{4 + c}", f"b_ps{c}", [P, PACK, QUARTER])
            for t in range(PACK):
                rows = slice(t * P, (t + 1) * P)
                product(b_ps[:, t, :], xq["b"][:, rows], xq_s["b"][:, rows], wq["wb"][:, cols], wq_s["wb"][:, cols])
            nc.vector.tensor_tensor(
                z2_woven[:, cols, :], b_ps[:].rearrange("p t n -> p n t"),
                gi_signed[:].unsqueeze(1).to_broadcast([P, QUARTER, PACK]), ALU.mult,
            )
            if c == 2:
                quantize(z2q[:, 0:HALF], z2q_s[:, 0:HALF], z2_woven[:, 0:HALF, :])
            else:
                larger_a(min(c, 2))
        quantize(z2q[:, HALF:N], z2q_s[:, HALF:N], z2_woven[:, HALF:N, :])
        larger_a(3, 0, HALF)
        larger_a(3, HALF, H)

        cv_win = [tile(f"cv_win{u}", [P, N], F32) for u in range(PACK)]
        cv_got = tile("cv_got", [P, PACK, N], F32)
        z_woven = [tile(f"z_woven{u}", [P, P, PACK], BF16) for u in range(PACK)]
        zq = [tile(f"zq{u}", [P, P], U32) for u in range(PACK)]
        zq_s = [tile(f"zq_s{u}", [P, P], U8) for u in range(PACK)]
        z_by_u = z_rows[:].rearrange("p t (m u) -> p u m t", u=PACK)
        cv_ps = []
        for u in range(PACK):
            if u in (1, 2):
                nc.scalar.copy(z_woven[u][:], z_by_u[:, u])
            else:
                nc.vector.tensor_copy(z_woven[u][:], z_by_u[:, u])
        for u in range(PACK):
            quantize(zq[u][:], zq_s[u][:], z_woven[u][:])
            cv_ps.append(bank(f"bank{u}", f"cv_ps{u}", [P, N]))
            product(cv_ps[u][:], zq[u][:], zq_s[u][:], z2q[:], z2q_s[:])

        out_rows = out_0.rearrange("(p u) n -> p u n", u=PACK)
        words = out_1[0].rearrange("p c r -> p (c r)").bitcast(I32)
        oq = tile("oq", [P, N], I32)
        oq_s = tile("oq_s", [P, N], U8)
        res = tile("res", [P, PACK, N], F32)

        def fetch(engine, u, lo, hi):
            gather(engine, cv_got[:, u, lo:hi], cv_win[u][:], nb_sb[:, lo // 16 : hi // 16])

        def larger_cv(u, lo, hi):
            nc.vector.tensor_tensor(res[:, u, lo:hi], cv_got[:, u, lo:hi], cv_win[u][:, lo:hi], ALU.max)

        def hand_out(lo, hi, engine):
            nc.sync.dma_start(out_rows[:, :, lo:hi], res[:, :, lo:hi])
            woven = tile(f"out_woven{lo}", [P, hi - lo, PACK], BF16)
            weave(engine, woven[:], res[:, :, lo:hi])
            quantize(oq[:, lo:hi], oq_s[:, lo:hi], woven[:])
            nc.sync.dma_start(words[:, lo:hi], oq[:, lo:hi])

        for u in range(PACK):
            if u % 2 == 0:
                nc.scalar.activation(cv_win[u][:], cv_ps[u][:], ACT.Copy, scale=0.0625)
            else:
                nc.vector.tensor_scalar(cv_win[u][:], cv_ps[u][:], 0.0625, None, ALU.mult)
        for u in range(PACK):
            fetch("scalar", u, 0, HALF)
            larger_cv(u, 0, HALF)
        hand_out(0, HALF, "vector")
        for u in (0, 1):
            fetch("vector" if u == 0 else "scalar", u, HALF, N)
            larger_cv(u, HALF, N)
        for lo, hi, engine in ((HALF, HALF + QUARTER, "scalar"), (HALF + QUARTER, N, "vector")):
            for u in (2, 3):
                fetch("scalar", u, lo, hi)
                larger_cv(u, lo, hi)
            hand_out(lo, hi, engine)
        for q in range(4):
            queue = nc.scalar if q % 2 == 0 else nc.sync
            queue.dma_start(out_2[0, 4 * q : 4 * q + 4, :].bitcast(I32), oq_s[32 * q : 32 * q + 4, :].bitcast(I32))
